import numpy as np
import ml_dtypes


def mxq(x, axis, fmt="e4m3"):
    dtype, down = {"e4m3": (ml_dtypes.float8_e4m3fn, 7), "e5m2": (ml_dtypes.float8_e5m2, 14)}[fmt]
    v = np.moveaxis(np.asarray(x, np.float32).astype(ml_dtypes.bfloat16).astype(np.float64), axis, -1)
    blocks = v.reshape(v.shape[:-1] + (-1, 32))
    amax = np.abs(blocks).max(-1, keepdims=True)
    byte = np.maximum(np.where(amax > 0, np.frexp(amax)[1] - 1 + 127, 0) - down, 1)
    scale = np.exp2(byte - 127.0)
    codes = (blocks / scale).astype(np.float32).astype(dtype).astype(np.float64)
    return np.moveaxis((codes * scale).reshape(v.shape), -1, axis)


WIDE = False


def mx_kscale(k):
    if not WIDE:
        return np.ones(k)
    levels = np.array([10, -10, 5, -5, 0])
    if k % 512:
        return np.exp2(np.random.permutation(np.resize(levels, k // 32))).repeat(32)
    a = np.empty((k // 512, 16))
    for p in range(k // 512):
        a[p, :8] = np.random.permutation(np.resize(levels, 8))
        for g in range(8):
            far = levels[np.abs(levels - a[p, g]) >= 10]
            a[p, g + 8] = far[np.random.randint(len(far))]
    return np.exp2(a.ravel()).repeat(32)


def f64(x):
    return np.asarray(x).astype(np.float64)


def striped(idx):
    return np.tile(idx.reshape(-1, 16).T, (8, 1)).astype(np.uint16)


def unstriped(offs):
    return offs[:16].T.reshape(-1).astype(np.int64)


def pack_weight(w):
    k, n = w.shape
    w = f64(np.asarray(w, np.float32).astype(ml_dtypes.bfloat16)).reshape(k // 32, 32, n)
    amax = np.abs(w).max(1)
    byte = np.clip(np.where(amax > 0, np.frexp(amax)[1] - 1 + 127 - 7, 1), 1, 254)
    scaled = (w * np.exp2(127.0 - byte)[:, None, :]).reshape(k, n).astype(np.float32)
    words = np.ascontiguousarray(scaled.reshape(k // 512, 128, 4, n).transpose(0, 1, 3, 2)).astype(ml_dtypes.float8_e4m3fn).view(np.uint8)
    return words, np.ascontiguousarray(byte.astype(np.uint8).reshape(k // 512, 16, n))


def unpack_weight(words, scales):
    g, p, n, _ = words.shape
    vals = np.ascontiguousarray(words).view(ml_dtypes.float8_e4m3fn).astype(np.float64) * np.repeat(np.exp2(scales.astype(np.float64) - 127.0), 8, axis=1)[..., None]
    return vals.transpose(0, 1, 3, 2).reshape(g * 512, n)


def sigmoid(v):
    return 1.0 / (1.0 + np.exp(-np.maximum(v, -700.0)))


K, T, S, N, D = 512, 2048, 512, 256, 2
P = 2 ** 7


def setup_inputs():
    n = np.random.standard_normal
    s = mx_kscale(K)[:, None]
    packed_xT = pack_weight(n((K, T)) * s)
    return {
        "x_words": packed_xT[0],
        "x_scales": packed_xT[1],
        "w1": (n((K, N)) / np.sqrt(K) / s).astype(np.float32),
        "gate": (np.tile(np.random.uniform(0.2, 0.5, (D, 1, S)), (1, P, 1))).astype(np.float32),
        "rate": (np.random.uniform(0.1, 0.8, (N, 1))).astype(np.float32),
        "offs": striped(np.random.permutation(T)[:S]),
        "pos1": striped(np.random.permutation(S)[:S]),
        "pos2": striped(np.random.permutation(S)[:S]),
    }


def reference(x_words, x_scales, w1, gate, rate, offs, pos1, pos2):
    xq = unpack_weight(x_words, x_scales)[:, unstriped(offs)]
    y = sigmoid(mxq(f64(w1), 0, "e4m3").T @ xq)
    dd = y[:, unstriped(pos1)] * f64(gate)[0, :1] + y[:, unstriped(pos2)] * f64(gate)[1, :1] - y
    rr = y - (y * y)
    return y + 0.5 * dd + f64(rate) * rr

@@ -1,0 +1,204 @@
+from contextlib import ExitStack
+
+import concourse.mybir as mybir
+from concourse.masks import make_identity
+
+K, T, S, N = 512, 2048, 512, 256
+FLOPS = 2 * K * N * S
+
+F32 = mybir.dt.float32
+BF16 = mybir.dt.bfloat16
+I32 = mybir.dt.int32
+U32 = mybir.dt.uint32
+U16 = mybir.dt.uint16
+U8 = mybir.dt.uint8
+FP8X4 = mybir.dt.float8_e4m3fn_x4
+ALU = mybir.AluOpType
+ACT = mybir.ActivationFunctionType
+
+P = 128
+PACK = 4
+LIST_COLS = S // 16
+BLOCKS = N // P
+HALVES = 2
+HALF = S // HALVES
+
+
+def tile_picked_ygread_fisher_p_kernel(
+    tc, x_words, x_scales, w1, gate, rate, offs, pos1, pos2, out
+):
+    nc = tc.nc
+
+    def cols(h):
+        return slice(h * HALF, (h + 1) * HALF)
+
+    def entries(h):
+        return slice(h * HALF // 16, (h + 1) * HALF // 16)
+
+    with ExitStack() as ctx:
+        keep = ctx.enter_context(tc.tile_pool(name="keep", bufs=1))
+        psum = ctx.enter_context(tc.psum_pool(name="psum", bufs=1))
+
+        offs_sb = keep.tile([P, LIST_COLS], U16, name="offs_sb")
+        pos1_sb = keep.tile([P, LIST_COLS], U16, name="pos1_sb")
+        pos2_sb = keep.tile([P, LIST_COLS], U16, name="pos2_sb")
+        table_scales = keep.tile([P, T], U8, name="table_scales", align_bytes=64)
+        table_words = keep.tile([P, T], I32, name="table_words", align_bytes=64)
+        w_raw = keep.tile([P, PACK, N], F32, name="w_raw")
+        identity = keep.tile([P, P], F32, name="identity")
+        gate_sb = [keep.tile([P, 2, HALF], F32, name=f"gate{h}") for h in range(HALVES)]
+        rate_sb = keep.tile([P, BLOCKS], F32, name="rate_sb")
+
+        nc.vector.memset(table_scales[:].bitcast(I32), 0)
+        nc.vector.memset(identity[:], 0.0)
+        make_identity(nc, identity[:], nomemset=True)
+        nc.sync.dma_start(w_raw[:], w1.rearrange("(p j) m -> p j m", j=PACK))
+        nc.sync.dma_start(offs_sb[:], offs)
+        for q in range(4):
+            nc.sync.dma_start(
+                table_scales[32 * q : 32 * q + 4, :].bitcast(I32),
+                x_scales[0, 4 * q : 4 * q + 4, :].bitcast(I32),
+            )
+        nc.sync.dma_start(table_words[:], x_words[0].rearrange("p c r -> p (c r)").bitcast(I32))
+        with nc.allow_non_contiguous_dma(reason="one rate for each partition and block"):
+            nc.sync.dma_start(rate_sb[:], rate.rearrange("(b p) o -> p (b o)", p=P))
+        nc.sync.dma_start(pos1_sb[:], pos1)
+        nc.sync.dma_start(pos2_sb[:], pos2)
+        for h in range(HALVES):
+            nc.sync.dma_start(gate_sb[h][:], gate[:, :, cols(h)].rearrange("d p j -> p d j"))
+
+        tilt = keep.tile([P, BLOCKS], F32, name="tilt")
+        shift = keep.tile([P, BLOCKS], F32, name="shift")
+        nc.gpsimd.tensor_scalar(tilt[:], rate_sb[:], -2.0, 0.0, ALU.mult, ALU.add)
+        nc.gpsimd.tensor_scalar(shift[:], rate_sb[:], 2.0, 1.0, ALU.mult, ALU.add)
+
+        w_codes = [keep.tile([P, P], U32, name=f"w_codes{b}", align_bytes=64) for b in range(BLOCKS)]
+        w_scales = [keep.tile([P, P], U8, name=f"w_scales{b}", align_bytes=64) for b in range(BLOCKS)]
+        w_grouped = [keep.tile([P, P, PACK], BF16, name=f"w_grouped{b}", align_bytes=64) for b in range(BLOCKS)]
+
+        def round_weights(b, copy):
+            copy(
+                w_grouped[b][:].rearrange("p (c i) j -> p c j i", i=4),
+                w_raw[:, :, b * P : (b + 1) * P].rearrange("p j (c i) -> p c j i", i=4),
+            )
+
+        def quantize_weights(b):
+            nc.vector.quantize_mx(
+                out=w_codes[b][:].bitcast(FP8X4),
+                scales=w_scales[b][:],
+                in_=w_grouped[b][:].rearrange("p m j -> p (m j)"),
+            )
+
+        round_weights(0, nc.vector.tensor_copy)
+        round_weights(1, nc.scalar.copy)
+        picked_scales = keep.tile([P, S], U8, name="picked_scales", align_bytes=64)
+        nc.vector.tensor_copy(picked_scales[:], table_scales[:].indirect(offs_sb[:]))
+
+        for b in range(BLOCKS):
+            quantize_weights(b)
+
+        picked_words = [keep.tile([P, HALF], U32, name=f"picked_words{h}", align_bytes=64) for h in range(HALVES)]
+        for h in range(HALVES):
+            nc.vector.tensor_copy(picked_words[h][:], table_words[:].bitcast(U32).indirect(offs_sb[:, entries(h)]))
+
+        y = [keep.tile([P, S], F32, name=f"y{b}") for b in range(BLOCKS)]
+        slope = [keep.tile([P, S], F32, name=f"slope{b}") for b in range(BLOCKS)]
+        logits = keep.tile([P, S], F32, name="logits")
+
+        def product(b, h):
+            acc = psum.tile([P, HALF], F32, name=f"acc{b}{h}")
+            nc.tensor.matmul_mx(
+                out=acc[:],
+                lhsT=w_codes[b][:].bitcast(FP8X4),
+                lhsT_scale=w_scales[b][:],
+                rhs=picked_words[h][:].bitcast(FP8X4),
+                rhs_scale=picked_scales[:, cols(h)],
+                start=True,
+                stop=True,
+            )
+            return acc
+
+        def make_slope(b, c):
+            nc.scalar.activation(
+                slope[b][:, c], y[b][:, c], ACT.Identity, bias=shift[:, b : b + 1], scale=tilt[:, b : b + 1]
+            )
+
+        for h in range(HALVES):
+            nc.scalar.activation(y[0][:, cols(h)], product(0, h)[:], ACT.Sigmoid)
+            make_slope(0, cols(h))
+            nc.vector.tensor_copy(logits[:, cols(h)], product(1, h)[:])
+
+        first = [keep.tile([P, S], F32, name=f"first{b}") for b in range(BLOCKS)]
+        second = [keep.tile([P, S], F32, name=f"second{b}") for b in range(BLOCKS)]
+        own = [keep.tile([P, S], F32, name=f"own{b}") for b in range(BLOCKS)]
+        both = keep.tile([P, S], F32, name="both")
+        result = [keep.tile([P, S], F32, name=f"result{b}") for b in range(BLOCKS)]
+        near = [keep.tile([P, S], F32, name=f"near{d}") for d in range(2)]
+        turned = keep.tile([P, S], F32, name="turned")
+
+        def fetch_on_scalar(d, pos_sb, h):
+            nc.scalar.activation(near[d][:, cols(h)], logits[:].indirect(pos_sb[:, entries(h)]), ACT.Sigmoid)
+
+        def fetch_on_vector(dst, d, pos_sb, h):
+            nc.vector.tensor_tensor(
+                dst[0][:, cols(h)], y[0][:].indirect(pos_sb[:, entries(h)]), gate_sb[h][:, d, :], ALU.mult
+            )
+
+        def own_term(b, c):
+            nc.vector.tensor_tensor(own[b][:, c], slope[b][:, c], y[b][:, c], ALU.mult)
+
+        def sum_turned(h):
+            bank = psum.tile([P, HALF], F32, name=f"sum{h}")
+            terms = (own[0], first[0], second[0])
+            for c in range(HALF // P):
+                for i, term in enumerate(terms):
+                    nc.tensor.matmul(
+                        bank[:, c * P : (c + 1) * P],
+                        term[:, h * HALF + c * P : h * HALF + (c + 1) * P],
+                        identity[:],
+                        start=(i == 0),
+                        stop=(i == len(terms) - 1),
+                        is_transpose=True,
+                    )
+            nc.scalar.copy(turned[:, cols(h)], bank[:])
+
+        def turn_back(h):
+            bank = psum.tile([P, HALF], F32, name=f"back{h}")
+            for c in range(HALF // P):
+                nc.tensor.transpose(
+                    bank[:, c * P : (c + 1) * P], turned[:, h * HALF + c * P : h * HALF + (c + 1) * P], identity[:]
+                )
+            nc.scalar.activation(result[0][:, cols(h)], bank[:], ACT.Copy, scale=0.5)
+            nc.sync.dma_start(out[0:P, cols(h)], result[0][:, cols(h)])
+
+        nc.scalar.activation(y[1][:], logits[:], ACT.Sigmoid)
+        whole = slice(0, S)
+        make_slope(1, whole)
+        for h in range(HALVES):
+            own_term(0, cols(h))
+            fetch_on_vector(first, 0, pos1_sb, h)
+            fetch_on_vector(second, 1, pos2_sb, h)
+        for h in range(HALVES):
+            fetch_on_scalar(0, pos1_sb, h)
+        sum_turned(0)
+        fetch_on_scalar(1, pos2_sb, 0)
+        sum_turned(1)
+        fetch_on_scalar(1, pos2_sb, 1)
+        for h in range(HALVES):
+            turn_back(h)
+
+        own_term(1, whole)
+        for h in range(HALVES):
+            nc.vector.tensor_tensor(first[1][:, cols(h)], near[0][:, cols(h)], gate_sb[h][:, 0, :], ALU.mult)
+        nc.vector.scalar_tensor_tensor(
+            second[1][:, cols(0)], near[1][:, cols(0)], 0.5, gate_sb[0][:, 1, :], ALU.mult, ALU.mult
+        )
+        nc.vector.tensor_tensor(both[:], first[1][:], own[1][:], ALU.add)
+        nc.vector.scalar_tensor_tensor(
+            second[1][:, cols(1)], near[1][:, cols(1)], 0.5, gate_sb[1][:, 1, :], ALU.mult, ALU.mult
+        )
+        for h in range(HALVES):
+            nc.vector.scalar_tensor_tensor(
+                result[1][:, cols(h)], both[:, cols(h)], 0.5, second[1][:, cols(h)], ALU.mult, ALU.add
+            )
+            nc.sync.dma_start(out[P : 2 * P, cols(h)], result[1][:, cols(h)])

@@ -46,7 +46,7 @@ def tile_picked_ygread_fisher_p_kernel(
         table_words = keep.tile([P, T], I32, name="table_words", align_bytes=64)
         w_raw = keep.tile([P, PACK, N], F32, name="w_raw")
         identity = keep.tile([P, P], F32, name="identity")
-        gate_sb = [keep.tile([P, 2, HALF], F32, name=f"gate{h}") for h in range(HALVES)]
+        gate_sb = [keep.tile([P, S], F32, name=f"gate{d}") for d in range(2)]
         rate_sb = keep.tile([P, BLOCKS], F32, name="rate_sb")
 
         nc.vector.memset(table_scales[:].bitcast(I32), 0)
@@ -63,9 +63,9 @@ def tile_picked_ygread_fisher_p_kernel(
         with nc.allow_non_contiguous_dma(reason="one rate for each partition and block"):
             nc.sync.dma_start(rate_sb[:], rate.rearrange("(b p) o -> p (b o)", p=P))
         nc.sync.dma_start(pos1_sb[:], pos1)
+        nc.sync.dma_start(gate_sb[0][:], gate[0])
         nc.sync.dma_start(pos2_sb[:], pos2)
-        for h in range(HALVES):
-            nc.sync.dma_start(gate_sb[h][:], gate[:, :, cols(h)].rearrange("d p j -> p d j"))
+        nc.sync.dma_start(gate_sb[1][:], gate[1])
 
         tilt = keep.tile([P, BLOCKS], F32, name="tilt")
         shift = keep.tile([P, BLOCKS], F32, name="shift")
@@ -141,7 +141,7 @@ def tile_picked_ygread_fisher_p_kernel(
 
         def fetch_on_vector(dst, d, pos_sb, h):
             nc.vector.tensor_tensor(
-                dst[0][:, cols(h)], y[0][:].indirect(pos_sb[:, entries(h)]), gate_sb[h][:, d, :], ALU.mult
+                dst[0][:, cols(h)], y[0][:].indirect(pos_sb[:, entries(h)]), gate_sb[d][:, cols(h)], ALU.mult
             )
 
         def own_term(b, c):
@@ -188,14 +188,13 @@ def tile_picked_ygread_fisher_p_kernel(
             turn_back(h)
 
         own_term(1, whole)
-        for h in range(HALVES):
-            nc.vector.tensor_tensor(first[1][:, cols(h)], near[0][:, cols(h)], gate_sb[h][:, 0, :], ALU.mult)
+        nc.vector.tensor_tensor(first[1][:], near[0][:], gate_sb[0][:], ALU.mult)
         nc.vector.scalar_tensor_tensor(
-            second[1][:, cols(0)], near[1][:, cols(0)], 0.5, gate_sb[0][:, 1, :], ALU.mult, ALU.mult
+            second[1][:, cols(0)], near[1][:, cols(0)], 0.5, gate_sb[1][:, cols(0)], ALU.mult, ALU.mult
         )
         nc.vector.tensor_tensor(both[:], first[1][:], own[1][:], ALU.add)
         nc.vector.scalar_tensor_tensor(
-            second[1][:, cols(1)], near[1][:, cols(1)], 0.5, gate_sb[1][:, 1, :], ALU.mult, ALU.mult
+            second[1][:, cols(1)], near[1][:, cols(1)], 0.5, gate_sb[1][:, cols(1)], ALU.mult, ALU.mult
         )
         for h in range(HALVES):
             nc.vector.scalar_tensor_tensor(

@@ -37,6 +37,7 @@ def tile_picked_ygread_fisher_p_kernel(
 
     with ExitStack() as ctx:
         keep = ctx.enter_context(tc.tile_pool(name="keep", bufs=1))
+        shared = ctx.enter_context(tc.tile_pool(name="shared", bufs=1))
         psum = ctx.enter_context(tc.psum_pool(name="psum", bufs=1))
 
         offs_sb = keep.tile([P, LIST_COLS], U16, name="offs_sb")
@@ -46,7 +47,7 @@ def tile_picked_ygread_fisher_p_kernel(
         table_words = keep.tile([P, T], I32, name="table_words", align_bytes=64)
         w_raw = keep.tile([P, PACK, N], F32, name="w_raw")
         identity = keep.tile([P, P], F32, name="identity")
-        gate_sb = [keep.tile([P, S], F32, name=f"gate{d}") for d in range(2)]
+        gate_sb = [keep.tile([P, 2, HALF], F32, name=f"gate{h}") for h in range(HALVES)]
         rate_sb = keep.tile([P, BLOCKS], F32, name="rate_sb")
 
         nc.vector.memset(table_scales[:].bitcast(I32), 0)
@@ -63,9 +64,10 @@ def tile_picked_ygread_fisher_p_kernel(
         with nc.allow_non_contiguous_dma(reason="one rate for each partition and block"):
             nc.sync.dma_start(rate_sb[:], rate.rearrange("(b p) o -> p (b o)", p=P))
         nc.sync.dma_start(pos1_sb[:], pos1)
-        nc.sync.dma_start(gate_sb[0][:], gate[0])
+        gate_rows = gate.rearrange("d p s -> p d s")
+        nc.sync.dma_start(gate_sb[0][:], gate_rows[:, :, cols(0)])
         nc.sync.dma_start(pos2_sb[:], pos2)
-        nc.sync.dma_start(gate_sb[1][:], gate[1])
+        nc.sync.dma_start(gate_sb[1][:], gate_rows[:, :, cols(1)])
 
         tilt = keep.tile([P, BLOCKS], F32, name="tilt")
         shift = keep.tile([P, BLOCKS], F32, name="shift")
@@ -101,7 +103,7 @@ def tile_picked_ygread_fisher_p_kernel(
         for h in range(HALVES):
             nc.vector.tensor_copy(picked_words[h][:], table_words[:].bitcast(U32).indirect(offs_sb[:, entries(h)]))
 
-        y = [keep.tile([P, S], F32, name=f"y{b}") for b in range(BLOCKS)]
+        y = [shared.tile([P, S], F32, name="y0", offset=4 * S - 64), keep.tile([P, S], F32, name="y1")]
         slope = [keep.tile([P, S], F32, name=f"slope{b}") for b in range(BLOCKS)]
         logits = keep.tile([P, S], F32, name="logits")
 
@@ -128,36 +130,40 @@ def tile_picked_ygread_fisher_p_kernel(
             make_slope(0, cols(h))
             nc.vector.tensor_copy(logits[:, cols(h)], product(1, h)[:])
 
-        first = [keep.tile([P, S], F32, name=f"first{b}") for b in range(BLOCKS)]
-        second = [keep.tile([P, S], F32, name=f"second{b}") for b in range(BLOCKS)]
-        own = [keep.tile([P, S], F32, name=f"own{b}") for b in range(BLOCKS)]
-        both = keep.tile([P, S], F32, name="both")
-        result = [keep.tile([P, S], F32, name=f"result{b}") for b in range(BLOCKS)]
-        near = [keep.tile([P, S], F32, name=f"near{d}") for d in range(2)]
-        turned = keep.tile([P, S], F32, name="turned")
+        def wide(name):
+            return keep.tile([P, S], F32, name=name)
 
-        def fetch_on_scalar(d, pos_sb, h):
-            nc.scalar.activation(near[d][:, cols(h)], logits[:].indirect(pos_sb[:, entries(h)]), ACT.Sigmoid)
+        def narrow(name, tag=None):
+            return keep.tile([P, HALF], F32, name=name, tag=tag or name)
 
-        def fetch_on_vector(dst, d, pos_sb, h):
-            nc.vector.tensor_tensor(
-                dst[0][:, cols(h)], y[0][:].indirect(pos_sb[:, entries(h)]), gate_sb[d][:, cols(h)], ALU.mult
-            )
+        own = [wide("own0"), wide("own1")]
+        first = shared.tile([P, S], F32, name="first", offset=8 * S - 128)
+        second = [shared.tile([P, HALF], F32, name="second0", offset=4 * S), narrow("second1")]
+        result = [wide("result0"), wide("result1")]
+        near_first, both, turned = wide("near_first"), wide("both"), wide("turned")
+        whole = slice(0, S)
+
+        def fetch_on_scalar(dst, pos_sb, h):
+            nc.scalar.activation(dst, logits[:].indirect(pos_sb[:, entries(h)]), ACT.Sigmoid)
+
+        def fetch_on_vector(d, pos_sb, h):
+            dst = narrow(f"weighed{d}{h}")
+            nc.vector.tensor_tensor(dst[:], y[0][:].indirect(pos_sb[:, entries(h)]), gate_sb[h][:, d, :], ALU.mult)
+            return dst
 
         def own_term(b, c):
             nc.vector.tensor_tensor(own[b][:, c], slope[b][:, c], y[b][:, c], ALU.mult)
 
-        def sum_turned(h):
+        def sum_turned(h, terms):
             bank = psum.tile([P, HALF], F32, name=f"sum{h}")
-            terms = (own[0], first[0], second[0])
-            for c in range(HALF // P):
-                for i, term in enumerate(terms):
+            for i, term in enumerate(terms):
+                for c in range(HALF // P):
                     nc.tensor.matmul(
                         bank[:, c * P : (c + 1) * P],
-                        term[:, h * HALF + c * P : h * HALF + (c + 1) * P],
+                        term[:, c * P : (c + 1) * P],
                         identity[:],
-                        start=(i == 0),
-                        stop=(i == len(terms) - 1),
+                        start=(i == 0 and c == 0),
+                        stop=(i == len(terms) - 1 and c == HALF // P - 1),
                         is_transpose=True,
                     )
             nc.scalar.copy(turned[:, cols(h)], bank[:])
@@ -171,33 +177,38 @@ def tile_picked_ygread_fisher_p_kernel(
             nc.scalar.activation(result[0][:, cols(h)], bank[:], ACT.Copy, scale=0.5)
             nc.sync.dma_start(out[0:P, cols(h)], result[0][:, cols(h)])
 
+        def weigh_second(h):
+            nc.vector.scalar_tensor_tensor(
+                second[h][:], near_second[h][:], 0.5, gate_sb[h][:, 1, :], ALU.mult, ALU.mult
+            )
+
+        def finish(h):
+            c = cols(h)
+            nc.vector.scalar_tensor_tensor(result[1][:, c], both[:, c], 0.5, second[h][:], ALU.mult, ALU.add)
+            nc.sync.dma_start(out[P : 2 * P, c], result[1][:, c])
+
         nc.scalar.activation(y[1][:], logits[:], ACT.Sigmoid)
-        whole = slice(0, S)
         make_slope(1, whole)
+        terms = []
         for h in range(HALVES):
             own_term(0, cols(h))
-            fetch_on_vector(first, 0, pos1_sb, h)
-            fetch_on_vector(second, 1, pos2_sb, h)
+            terms.append((own[0][:, cols(h)], fetch_on_vector(0, pos1_sb, h), fetch_on_vector(1, pos2_sb, h)))
         for h in range(HALVES):
-            fetch_on_scalar(0, pos1_sb, h)
-        sum_turned(0)
-        fetch_on_scalar(1, pos2_sb, 0)
-        sum_turned(1)
-        fetch_on_scalar(1, pos2_sb, 1)
+            fetch_on_scalar(near_first[:, cols(h)], pos1_sb, h)
+        near_second = [narrow("near_second0")]
+        fetch_on_scalar(near_second[0][:], pos2_sb, 0)
+        for h in range(HALVES):
+            sum_turned(h, terms[h])
+        near_second.append(narrow("near_second1", "weighed10"))
+        fetch_on_scalar(near_second[1][:], pos2_sb, 1)
         for h in range(HALVES):
             turn_back(h)
 
         own_term(1, whole)
-        nc.vector.tensor_tensor(first[1][:], near[0][:], gate_sb[0][:], ALU.mult)
-        nc.vector.scalar_tensor_tensor(
-            second[1][:, cols(0)], near[1][:, cols(0)], 0.5, gate_sb[1][:, cols(0)], ALU.mult, ALU.mult
-        )
-        nc.vector.tensor_tensor(both[:], first[1][:], own[1][:], ALU.add)
-        nc.vector.scalar_tensor_tensor(
-            second[1][:, cols(1)], near[1][:, cols(1)], 0.5, gate_sb[1][:, cols(1)], ALU.mult, ALU.mult
-        )
         for h in range(HALVES):
-            nc.vector.scalar_tensor_tensor(
-                result[1][:, cols(h)], both[:, cols(h)], 0.5, second[1][:, cols(h)], ALU.mult, ALU.add
-            )
-            nc.sync.dma_start(out[P : 2 * P, cols(h)], result[1][:, cols(h)])
+            nc.vector.tensor_tensor(first[:, cols(h)], near_first[:, cols(h)], gate_sb[h][:, 0, :], ALU.mult)
+        weigh_second(0)
+        nc.vector.tensor_tensor(both[:], first[:], own[1][:], ALU.add)
+        weigh_second(1)
+        for h in range(HALVES):
+            finish(h)

@@ -74,6 +74,13 @@ def tile_picked_ygread_fisher_p_kernel(
         nc.gpsimd.tensor_scalar(tilt[:], rate_sb[:], -2.0, 0.0, ALU.mult, ALU.add)
         nc.gpsimd.tensor_scalar(shift[:], rate_sb[:], 2.0, 1.0, ALU.mult, ALU.add)
 
+        minus_rate = keep.tile([P, 1], F32, name="minus_rate")
+        half_rate = keep.tile([P, 1], F32, name="half_rate")
+        centre = keep.tile([P, 1], F32, name="centre")
+        nc.gpsimd.tensor_scalar(minus_rate[:], rate_sb[:, 0:1], -1.0, 0.0, ALU.mult, ALU.add)
+        nc.gpsimd.tensor_scalar(half_rate[:], rate_sb[:, 0:1], 0.5, 0.0, ALU.mult, ALU.add)
+        nc.gpsimd.memset(centre[:], -0.5)
+
         w_codes = [keep.tile([P, P], U32, name=f"w_codes{b}", align_bytes=64) for b in range(BLOCKS)]
         w_scales = [keep.tile([P, P], U8, name=f"w_scales{b}", align_bytes=64) for b in range(BLOCKS)]
         w_grouped = [keep.tile([P, P, PACK], BF16, name=f"w_grouped{b}", align_bytes=64) for b in range(BLOCKS)]
@@ -127,7 +134,8 @@ def tile_picked_ygread_fisher_p_kernel(
 
         for h in range(HALVES):
             nc.scalar.activation(y[0][:, cols(h)], product(0, h)[:], ACT.Sigmoid)
-            make_slope(0, cols(h))
+            if h == 0:
+                make_slope(0, cols(h))
             nc.vector.tensor_copy(logits[:, cols(h)], product(1, h)[:])
 
         def wide(name):
@@ -166,7 +174,7 @@ def tile_picked_ygread_fisher_p_kernel(
                         stop=(i == len(terms) - 1 and c == HALF // P - 1),
                         is_transpose=True,
                     )
-            nc.scalar.copy(turned[:, cols(h)], bank[:])
+            nc.scalar.activation(turned[:, cols(h)], bank[:], ACT.Copy, scale=0.5)
 
         def turn_back(h):
             bank = psum.tile([P, HALF], F32, name=f"back{h}")
@@ -174,8 +182,7 @@ def tile_picked_ygread_fisher_p_kernel(
                 nc.tensor.transpose(
                     bank[:, c * P : (c + 1) * P], turned[:, h * HALF + c * P : h * HALF + (c + 1) * P], identity[:]
                 )
-            nc.scalar.activation(result[0][:, cols(h)], bank[:], ACT.Copy, scale=0.5)
-            nc.sync.dma_start(out[0:P, cols(h)], result[0][:, cols(h)])
+            return bank
 
         def weigh_second(h):
             nc.vector.scalar_tensor_tensor(
@@ -189,20 +196,29 @@ def tile_picked_ygread_fisher_p_kernel(
 
         nc.scalar.activation(y[1][:], logits[:], ACT.Sigmoid)
         make_slope(1, whole)
-        terms = []
-        for h in range(HALVES):
-            own_term(0, cols(h))
-            terms.append((own[0][:, cols(h)], fetch_on_vector(0, pos1_sb, h), fetch_on_vector(1, pos2_sb, h)))
+        own_term(0, cols(0))
+        terms = [
+            (own[0][:, cols(0)], fetch_on_vector(0, pos1_sb, 0), fetch_on_vector(1, pos2_sb, 0)),
+            (
+                half_rate[:].to_broadcast([P, HALF]),
+                y[0][:, cols(1)],
+                fetch_on_vector(0, pos1_sb, 1),
+                fetch_on_vector(1, pos2_sb, 1),
+            ),
+        ]
         for h in range(HALVES):
             fetch_on_scalar(near_first[:, cols(h)], pos1_sb, h)
         near_second = [narrow("near_second0")]
         fetch_on_scalar(near_second[0][:], pos2_sb, 0)
         for h in range(HALVES):
             sum_turned(h, terms[h])
-        near_second.append(narrow("near_second1", "weighed10"))
+        near_second.append(narrow("near_second1", "weighed11"))
         fetch_on_scalar(near_second[1][:], pos2_sb, 1)
-        for h in range(HALVES):
-            turn_back(h)
+        nc.scalar.copy(result[0][:, cols(0)], turn_back(0)[:])
+        nc.sync.dma_start(out[0:P, cols(0)], result[0][:, cols(0)])
+        linear = turn_back(1)
+        square = narrow("square")
+        nc.scalar.activation(square[:], y[0][:, cols(1)], ACT.Square, bias=centre[:])
 
         own_term(1, whole)
         for h in range(HALVES):
@@ -210,5 +226,7 @@ def tile_picked_ygread_fisher_p_kernel(
         weigh_second(0)
         nc.vector.tensor_tensor(both[:], first[:], own[1][:], ALU.add)
         weigh_second(1)
-        for h in range(HALVES):
-            finish(h)
+        finish(0)
+        nc.vector.scalar_tensor_tensor(result[0][:, cols(1)], square[:], minus_rate[:], linear[:], ALU.mult, ALU.add)
+        nc.sync.dma_start(out[0:P, cols(1)], result[0][:, cols(1)])
+        finish(1)

@@ -37,7 +37,6 @@ def tile_picked_ygread_fisher_p_kernel(
 
     with ExitStack() as ctx:
         keep = ctx.enter_context(tc.tile_pool(name="keep", bufs=1))
-        shared = ctx.enter_context(tc.tile_pool(name="shared", bufs=1))
         psum = ctx.enter_context(tc.psum_pool(name="psum", bufs=1))
 
         offs_sb = keep.tile([P, LIST_COLS], U16, name="offs_sb")
@@ -47,7 +46,7 @@ def tile_picked_ygread_fisher_p_kernel(
         table_words = keep.tile([P, T], I32, name="table_words", align_bytes=64)
         w_raw = keep.tile([P, PACK, N], F32, name="w_raw")
         identity = keep.tile([P, P], F32, name="identity")
-        gate_sb = [keep.tile([P, 2, HALF], F32, name=f"gate{h}") for h in range(HALVES)]
+        gate_sb = keep.tile([P, 2, S], F32, name="gate_sb")
         rate_sb = keep.tile([P, BLOCKS], F32, name="rate_sb")
 
         nc.vector.memset(table_scales[:].bitcast(I32), 0)
@@ -64,21 +63,14 @@ def tile_picked_ygread_fisher_p_kernel(
         with nc.allow_non_contiguous_dma(reason="one rate for each partition and block"):
             nc.sync.dma_start(rate_sb[:], rate.rearrange("(b p) o -> p (b o)", p=P))
         nc.sync.dma_start(pos1_sb[:], pos1)
-        gate_rows = gate.rearrange("d p s -> p d s")
-        nc.sync.dma_start(gate_sb[0][:], gate_rows[:, :, cols(0)])
         nc.sync.dma_start(pos2_sb[:], pos2)
-        nc.sync.dma_start(gate_sb[1][:], gate_rows[:, :, cols(1)])
+        nc.sync.dma_start(gate_sb[:], gate.rearrange("d p s -> p d s"))
 
-        tilt = keep.tile([P, BLOCKS], F32, name="tilt")
-        shift = keep.tile([P, BLOCKS], F32, name="shift")
-        nc.gpsimd.tensor_scalar(tilt[:], rate_sb[:], -2.0, 0.0, ALU.mult, ALU.add)
-        nc.gpsimd.tensor_scalar(shift[:], rate_sb[:], 2.0, 1.0, ALU.mult, ALU.add)
-
-        minus_rate = keep.tile([P, 1], F32, name="minus_rate")
-        half_rate = keep.tile([P, 1], F32, name="half_rate")
+        minus_rate = keep.tile([P, BLOCKS], F32, name="minus_rate")
+        half_rate = keep.tile([P, BLOCKS], F32, name="half_rate")
         centre = keep.tile([P, 1], F32, name="centre")
-        nc.gpsimd.tensor_scalar(minus_rate[:], rate_sb[:, 0:1], -1.0, 0.0, ALU.mult, ALU.add)
-        nc.gpsimd.tensor_scalar(half_rate[:], rate_sb[:, 0:1], 0.5, 0.0, ALU.mult, ALU.add)
+        nc.gpsimd.tensor_scalar(minus_rate[:], rate_sb[:], -1.0, 0.0, ALU.mult, ALU.add)
+        nc.gpsimd.tensor_scalar(half_rate[:], rate_sb[:], 0.5, 0.0, ALU.mult, ALU.add)
         nc.gpsimd.memset(centre[:], -0.5)
 
         w_codes = [keep.tile([P, P], U32, name=f"w_codes{b}", align_bytes=64) for b in range(BLOCKS)]
@@ -102,7 +94,6 @@ def tile_picked_ygread_fisher_p_kernel(
         round_weights(1, nc.scalar.copy)
         picked_scales = keep.tile([P, S], U8, name="picked_scales", align_bytes=64)
         nc.vector.tensor_copy(picked_scales[:], table_scales[:].indirect(offs_sb[:]))
-
         for b in range(BLOCKS):
             quantize_weights(b)
 
@@ -110,123 +101,101 @@ def tile_picked_ygread_fisher_p_kernel(
         for h in range(HALVES):
             nc.vector.tensor_copy(picked_words[h][:], table_words[:].bitcast(U32).indirect(offs_sb[:, entries(h)]))
 
-        y = [shared.tile([P, S], F32, name="y0", offset=4 * S - 64), keep.tile([P, S], F32, name="y1")]
-        slope = [keep.tile([P, S], F32, name=f"slope{b}") for b in range(BLOCKS)]
-        logits = keep.tile([P, S], F32, name="logits")
-
-        def product(b, h):
-            acc = psum.tile([P, HALF], F32, name=f"acc{b}{h}")
-            nc.tensor.matmul_mx(
-                out=acc[:],
-                lhsT=w_codes[b][:].bitcast(FP8X4),
-                lhsT_scale=w_scales[b][:],
-                rhs=picked_words[h][:].bitcast(FP8X4),
-                rhs_scale=picked_scales[:, cols(h)],
-                start=True,
-                stop=True,
-            )
-            return acc
-
-        def make_slope(b, c):
-            nc.scalar.activation(
-                slope[b][:, c], y[b][:, c], ACT.Identity, bias=shift[:, b : b + 1], scale=tilt[:, b : b + 1]
-            )
-
+        y = [keep.tile([P, S], F32, name=f"y{b}") for b in range(BLOCKS)]
         for h in range(HALVES):
-            nc.scalar.activation(y[0][:, cols(h)], product(0, h)[:], ACT.Sigmoid)
-            if h == 0:
-                make_slope(0, cols(h))
-            nc.vector.tensor_copy(logits[:, cols(h)], product(1, h)[:])
+            for b in range(BLOCKS):
+                acc = psum.tile([P, HALF], F32, name=f"acc{b}{h}", tag=f"bank{b}{h}")
+                nc.tensor.matmul_mx(
+                    out=acc[:],
+                    lhsT=w_codes[b][:].bitcast(FP8X4),
+                    lhsT_scale=w_scales[b][:],
+                    rhs=picked_words[h][:].bitcast(FP8X4),
+                    rhs_scale=picked_scales[:, cols(h)],
+                    start=True,
+                    stop=True,
+                )
+                nc.scalar.activation(y[b][:, cols(h)], acc[:], ACT.Sigmoid)
 
-        def wide(name):
-            return keep.tile([P, S], F32, name=name)
+        pos_sb = [pos1_sb, pos2_sb]
 
         def narrow(name, tag=None):
             return keep.tile([P, HALF], F32, name=name, tag=tag or name)
 
-        own = [wide("own0"), wide("own1")]
-        first = shared.tile([P, S], F32, name="first", offset=8 * S - 128)
-        second = [shared.tile([P, HALF], F32, name="second0", offset=4 * S), narrow("second1")]
-        result = [wide("result0"), wide("result1")]
-        near_first, both, turned = wide("near_first"), wide("both"), wide("turned")
-        whole = slice(0, S)
-
-        def fetch_on_scalar(dst, pos_sb, h):
-            nc.scalar.activation(dst, logits[:].indirect(pos_sb[:, entries(h)]), ACT.Sigmoid)
-
-        def fetch_on_vector(d, pos_sb, h):
-            dst = narrow(f"weighed{d}{h}")
-            nc.vector.tensor_tensor(dst[:], y[0][:].indirect(pos_sb[:, entries(h)]), gate_sb[h][:, d, :], ALU.mult)
+        def fetch_weighed(b, h, d):
+            dst = narrow(f"weighed{b}{h}{d}")
+            nc.vector.tensor_tensor(dst[:], y[b][:].indirect(pos_sb[d][:, entries(h)]), gate_sb[:, d, cols(h)], ALU.mult)
             return dst
 
-        def own_term(b, c):
-            nc.vector.tensor_tensor(own[b][:, c], slope[b][:, c], y[b][:, c], ALU.mult)
+        def fetch(b, h, d, tag=None):
+            dst = narrow(f"near{b}{h}{d}", tag)
+            nc.scalar.activation(dst[:], y[b][:].indirect(pos_sb[d][:, entries(h)]), ACT.Copy)
+            return dst
 
-        def sum_turned(h, terms):
-            bank = psum.tile([P, HALF], F32, name=f"sum{h}")
-            for i, term in enumerate(terms):
-                for c in range(HALF // P):
-                    nc.tensor.matmul(
-                        bank[:, c * P : (c + 1) * P],
-                        term[:, c * P : (c + 1) * P],
-                        identity[:],
-                        start=(i == 0 and c == 0),
-                        stop=(i == len(terms) - 1 and c == HALF // P - 1),
-                        is_transpose=True,
-                    )
-            nc.scalar.activation(turned[:, cols(h)], bank[:], ACT.Copy, scale=0.5)
+        def weigh(near, b, h, d, factor):
+            dst = narrow(f"weighed{b}{h}{d}")
+            nc.vector.scalar_tensor_tensor(dst[:], near[:], factor, gate_sb[:, d, cols(h)], ALU.mult, ALU.mult)
+            return dst
 
-        def turn_back(h):
-            bank = psum.tile([P, HALF], F32, name=f"back{h}")
+        def bend(b, h):
+            dst = narrow(f"bend{b}{h}")
+            nc.vector.scalar_tensor_tensor(dst[:], y[b][:, cols(h)], -1.0, y[b][:, cols(h)], ALU.add, ALU.mult)
+            return dst
+
+        def square(b, h, tag=None):
+            dst = narrow(f"square{b}{h}", tag)
+            nc.scalar.activation(dst[:], y[b][:, cols(h)], ACT.Square, bias=centre[:])
+            return dst
+
+        def add_turned(bank, term, first=False, last=False):
             for c in range(HALF // P):
-                nc.tensor.transpose(
-                    bank[:, c * P : (c + 1) * P], turned[:, h * HALF + c * P : h * HALF + (c + 1) * P], identity[:]
+                nc.tensor.matmul(
+                    bank[:, c * P : (c + 1) * P],
+                    term[:, c * P : (c + 1) * P],
+                    identity[:],
+                    start=(first and c == 0),
+                    stop=(last and c == HALF // P - 1),
+                    is_transpose=True,
                 )
-            return bank
 
-        def weigh_second(h):
-            nc.vector.scalar_tensor_tensor(
-                second[h][:], near_second[h][:], 0.5, gate_sb[h][:, 1, :], ALU.mult, ALU.mult
-            )
+        def turn_back(bank, b, h, tag):
+            turned = narrow(f"turned{b}{h}")
+            nc.scalar.activation(turned[:], bank[:], ACT.Copy, scale=0.5)
+            back = psum.tile([P, HALF], F32, name=f"back{b}{h}", tag=tag)
+            for c in range(HALF // P):
+                nc.tensor.transpose(back[:, c * P : (c + 1) * P], turned[:, c * P : (c + 1) * P], identity[:])
+            return back
 
-        def finish(h):
-            c = cols(h)
-            nc.vector.scalar_tensor_tensor(result[1][:, c], both[:, c], 0.5, second[h][:], ALU.mult, ALU.add)
-            nc.sync.dma_start(out[P : 2 * P, c], result[1][:, c])
+        def store(result, b, h):
+            nc.sync.dma_start(out[b * P : (b + 1) * P, cols(h)], result[:])
 
-        nc.scalar.activation(y[1][:], logits[:], ACT.Sigmoid)
-        make_slope(1, whole)
-        own_term(0, cols(0))
-        terms = [
-            (own[0][:, cols(0)], fetch_on_vector(0, pos1_sb, 0), fetch_on_vector(1, pos2_sb, 0)),
-            (
-                half_rate[:].to_broadcast([P, HALF]),
-                y[0][:, cols(1)],
-                fetch_on_vector(0, pos1_sb, 1),
-                fetch_on_vector(1, pos2_sb, 1),
-            ),
-        ]
+        def finish_turned(back, curve, b, h):
+            result = narrow(f"result{b}{h}")
+            nc.vector.scalar_tensor_tensor(result[:], curve[:], minus_rate[:, b : b + 1], back[:], ALU.mult, ALU.add)
+            store(result, b, h)
+
+        sums = {(b, h): psum.tile([P, HALF], F32, name=f"sum{b}{h}") for h in range(HALVES) for b in range(BLOCKS)}
+        curve = {(b, 0): bend(b, 0) for b in range(BLOCKS)}
+        for b in range(BLOCKS):
+            add_turned(sums[b, 0], y[b][:, cols(0)], first=True)
+        for b in range(BLOCKS):
+            add_turned(sums[b, 1], y[b][:, cols(1)], first=True)
+        add_turned(sums[0, 0], fetch_weighed(0, 0, 0))
+        add_turned(sums[1, 0], fetch_weighed(1, 0, 0))
+        add_turned(sums[0, 0], weigh(fetch(0, 0, 1), 0, 0, 1, 1.0), last=True)
+        add_turned(sums[1, 0], weigh(fetch(1, 0, 1), 1, 0, 1, 1.0), last=True)
+        for b in range(BLOCKS):
+            add_turned(sums[b, 1], half_rate[:, b : b + 1].to_broadcast([P, HALF]))
+        add_turned(sums[0, 1], fetch_weighed(0, 1, 0))
+        add_turned(sums[0, 1], weigh(fetch(0, 1, 1), 0, 1, 1, 1.0), last=True)
+        add_turned(sums[1, 1], fetch_weighed(1, 1, 0))
+        add_turned(sums[1, 1], weigh(fetch(1, 1, 1), 1, 1, 1, 1.0), last=True)
+        back = {}
+        back[0, 0] = turn_back(sums[0, 0], 0, 0, "bank00")
+        back[1, 0] = turn_back(sums[1, 0], 1, 0, "bank10")
+        back[0, 1] = turn_back(sums[0, 1], 0, 1, "bank01")
+        curve[0, 1] = square(0, 1, "weighed011")
+        back[1, 1] = turn_back(sums[1, 1], 1, 1, "bank11")
+        curve[1, 1] = square(1, 1, "weighed111")
         for h in range(HALVES):
-            fetch_on_scalar(near_first[:, cols(h)], pos1_sb, h)
-        near_second = [narrow("near_second0")]
-        fetch_on_scalar(near_second[0][:], pos2_sb, 0)
-        for h in range(HALVES):
-            sum_turned(h, terms[h])
-        near_second.append(narrow("near_second1", "weighed11"))
-        fetch_on_scalar(near_second[1][:], pos2_sb, 1)
-        nc.scalar.copy(result[0][:, cols(0)], turn_back(0)[:])
-        nc.sync.dma_start(out[0:P, cols(0)], result[0][:, cols(0)])
-        linear = turn_back(1)
-        square = narrow("square")
-        nc.scalar.activation(square[:], y[0][:, cols(1)], ACT.Square, bias=centre[:])
-
-        own_term(1, whole)
-        for h in range(HALVES):
-            nc.vector.tensor_tensor(first[:, cols(h)], near_first[:, cols(h)], gate_sb[h][:, 0, :], ALU.mult)
-        weigh_second(0)
-        nc.vector.tensor_tensor(both[:], first[:], own[1][:], ALU.add)
-        weigh_second(1)
-        finish(0)
-        nc.vector.scalar_tensor_tensor(result[0][:, cols(1)], square[:], minus_rate[:], linear[:], ALU.mult, ALU.add)
-        nc.sync.dma_start(out[0:P, cols(1)], result[0][:, cols(1)])
-        finish(1)
+            for b in range(BLOCKS):
+                finish_turned(back[b, h], curve[b, h], b, h)

@@ -68,9 +68,11 @@ def tile_picked_ygread_fisher_p_kernel(
 
         minus_rate = keep.tile([P, BLOCKS], F32, name="minus_rate")
         half_rate = keep.tile([P, BLOCKS], F32, name="half_rate")
+        shift = keep.tile([P, BLOCKS], F32, name="shift")
         centre = keep.tile([P, 1], F32, name="centre")
         nc.gpsimd.tensor_scalar(minus_rate[:], rate_sb[:], -1.0, 0.0, ALU.mult, ALU.add)
         nc.gpsimd.tensor_scalar(half_rate[:], rate_sb[:], 0.5, 0.0, ALU.mult, ALU.add)
+        nc.gpsimd.tensor_scalar(shift[:], rate_sb[:], 1.0, 0.5, ALU.mult, ALU.add)
         nc.gpsimd.memset(centre[:], -0.5)
 
         w_codes = [keep.tile([P, P], U32, name=f"w_codes{b}", align_bytes=64) for b in range(BLOCKS)]
@@ -173,29 +175,51 @@ def tile_picked_ygread_fisher_p_kernel(
             nc.vector.scalar_tensor_tensor(result[:], curve[:], minus_rate[:, b : b + 1], back[:], ALU.mult, ALU.add)
             store(result, b, h)
 
-        sums = {(b, h): psum.tile([P, HALF], F32, name=f"sum{b}{h}") for h in range(HALVES) for b in range(BLOCKS)}
+        def make_slope(b, h, tag=None):
+            dst = narrow(f"slope{b}{h}", tag)
+            nc.scalar.activation(
+                dst[:], y[b][:, cols(h)], ACT.Identity, bias=shift[:, b : b + 1], scale=minus_rate[:, b : b + 1]
+            )
+            return dst
+
+        def make_own(slope, b, h, tag=None):
+            dst = narrow(f"own{b}{h}", tag)
+            nc.vector.tensor_tensor(dst[:], slope[:], y[b][:, cols(h)], ALU.mult)
+            return dst
+
+        def add_terms(first, second, b, h, tag=None):
+            dst = narrow(f"both{b}{h}", tag)
+            nc.vector.tensor_tensor(dst[:], first[:], second[:], ALU.add)
+            return dst
+
+        def finish_halved(term, rest, b, h):
+            result = narrow(f"result{b}{h}")
+            nc.vector.scalar_tensor_tensor(result[:], term[:], 0.5, rest[:], ALU.mult, ALU.add)
+            store(result, b, h)
+
+        sums = {q: psum.tile([P, HALF], F32, name=f"sum{q[0]}{q[1]}") for q in ((0, 0), (1, 0), (0, 1))}
         curve = {(b, 0): bend(b, 0) for b in range(BLOCKS)}
         for b in range(BLOCKS):
             add_turned(sums[b, 0], y[b][:, cols(0)], first=True)
-        for b in range(BLOCKS):
-            add_turned(sums[b, 1], y[b][:, cols(1)], first=True)
+        add_turned(sums[0, 1], y[0][:, cols(1)], first=True)
+        add_turned(sums[0, 1], half_rate[:, 0:1].to_broadcast([P, HALF]))
         add_turned(sums[0, 0], fetch_weighed(0, 0, 0))
         add_turned(sums[1, 0], fetch_weighed(1, 0, 0))
         add_turned(sums[0, 0], weigh(fetch(0, 0, 1), 0, 0, 1, 1.0), last=True)
         add_turned(sums[1, 0], weigh(fetch(1, 0, 1), 1, 0, 1, 1.0), last=True)
-        for b in range(BLOCKS):
-            add_turned(sums[b, 1], half_rate[:, b : b + 1].to_broadcast([P, HALF]))
         add_turned(sums[0, 1], fetch_weighed(0, 1, 0))
         add_turned(sums[0, 1], weigh(fetch(0, 1, 1), 0, 1, 1, 1.0), last=True)
-        add_turned(sums[1, 1], fetch_weighed(1, 1, 0))
-        add_turned(sums[1, 1], weigh(fetch(1, 1, 1), 1, 1, 1, 1.0), last=True)
-        back = {}
-        back[0, 0] = turn_back(sums[0, 0], 0, 0, "bank00")
-        back[1, 0] = turn_back(sums[1, 0], 1, 0, "bank10")
-        back[0, 1] = turn_back(sums[0, 1], 0, 1, "bank01")
+        near11 = fetch(1, 1, 0)
+        back00 = turn_back(sums[0, 0], 0, 0, "bank00")
+        back10 = turn_back(sums[1, 0], 1, 0, "bank10")
+        slope11 = make_slope(1, 1, "weighed101")
+        back01 = turn_back(sums[0, 1], 0, 1, "bank01")
         curve[0, 1] = square(0, 1, "weighed011")
-        back[1, 1] = turn_back(sums[1, 1], 1, 1, "bank11")
-        curve[1, 1] = square(1, 1, "weighed111")
-        for h in range(HALVES):
-            for b in range(BLOCKS):
-                finish_turned(back[b, h], curve[b, h], b, h)
+        first11 = weigh(near11, 1, 1, 0, 0.5)
+        second11 = fetch_weighed(1, 1, 1)
+        own11 = make_own(slope11, 1, 1)
+        finish_turned(back00, curve[0, 0], 0, 0)
+        both11 = add_terms(first11, own11, 1, 1)
+        finish_turned(back10, curve[1, 0], 1, 0)
+        finish_halved(second11, both11, 1, 1)
+        finish_turned(back01, curve[0, 1], 0, 1)

@@ -159,8 +159,8 @@ def tile_picked_ygread_fisher_p_kernel(
                     is_transpose=True,
                 )
 
-        def turn_back(bank, b, h, tag):
-            turned = narrow(f"turned{b}{h}")
+        def turn_back(bank, b, h, tag, buffer=None):
+            turned = narrow(f"turned{b}{h}", buffer)
             nc.scalar.activation(turned[:], bank[:], ACT.Copy, scale=0.5)
             back = psum.tile([P, HALF], F32, name=f"back{b}{h}", tag=tag)
             for c in range(HALF // P):
@@ -210,16 +210,16 @@ def tile_picked_ygread_fisher_p_kernel(
         add_turned(sums[0, 1], fetch_weighed(0, 1, 0))
         add_turned(sums[0, 1], weigh(fetch(0, 1, 1), 0, 1, 1, 1.0), last=True)
         near11 = fetch(1, 1, 0)
-        back00 = turn_back(sums[0, 0], 0, 0, "bank00")
-        back10 = turn_back(sums[1, 0], 1, 0, "bank10")
-        slope11 = make_slope(1, 1, "weighed101")
+        slope11 = make_slope(1, 1)
+        first11 = weigh(near11, 1, 1, 0, 0.5)
+        back00 = turn_back(sums[0, 0], 0, 0, "bank00", "near011")
+        back10 = turn_back(sums[1, 0], 1, 0, "bank10", "near110")
         back01 = turn_back(sums[0, 1], 0, 1, "bank01")
         curve[0, 1] = square(0, 1, "weighed011")
-        first11 = weigh(near11, 1, 1, 0, 0.5)
+        own11 = make_own(slope11, 1, 1, "near001")
         second11 = fetch_weighed(1, 1, 1)
-        own11 = make_own(slope11, 1, 1)
-        finish_turned(back00, curve[0, 0], 0, 0)
         both11 = add_terms(first11, own11, 1, 1)
-        finish_turned(back10, curve[1, 0], 1, 0)
+        finish_turned(back00, curve[0, 0], 0, 0)
         finish_halved(second11, both11, 1, 1)
+        finish_turned(back10, curve[1, 0], 1, 0)
         finish_turned(back01, curve[0, 1], 0, 1)

@@ -197,29 +197,47 @@ def tile_picked_ygread_fisher_p_kernel(
             nc.vector.scalar_tensor_tensor(result[:], term[:], 0.5, rest[:], ALU.mult, ALU.add)
             store(result, b, h)
 
-        sums = {q: psum.tile([P, HALF], F32, name=f"sum{q[0]}{q[1]}") for q in ((0, 0), (1, 0), (0, 1))}
+        sums = {b: psum.tile([P, HALF], F32, name=f"sum{b}") for b in range(BLOCKS)}
+        late = [psum.tile([P, P], F32, name=f"late{c}") for c in range(HALF // P)]
+        def add_late(term, first=False, last=False):
+            for c in range(HALF // P):
+                nc.tensor.matmul(late[c][:], term[:, c * P : (c + 1) * P], identity[:], start=first, stop=last, is_transpose=True)
         curve = {(b, 0): bend(b, 0) for b in range(BLOCKS)}
         for b in range(BLOCKS):
-            add_turned(sums[b, 0], y[b][:, cols(0)], first=True)
-        add_turned(sums[0, 1], y[0][:, cols(1)], first=True)
-        add_turned(sums[0, 1], half_rate[:, 0:1].to_broadcast([P, HALF]))
-        add_turned(sums[0, 0], fetch_weighed(0, 0, 0))
-        add_turned(sums[1, 0], fetch_weighed(1, 0, 0))
-        add_turned(sums[0, 0], weigh(fetch(0, 0, 1), 0, 0, 1, 1.0), last=True)
-        add_turned(sums[1, 0], weigh(fetch(1, 0, 1), 1, 0, 1, 1.0), last=True)
-        add_turned(sums[0, 1], fetch_weighed(0, 1, 0))
-        add_turned(sums[0, 1], weigh(fetch(0, 1, 1), 0, 1, 1, 1.0), last=True)
+            add_turned(sums[b], y[b][:, cols(0)], first=True)
+        add_late(y[0][:, cols(1)], first=True)
+        add_late(half_rate[:, 0:1].to_broadcast([P, HALF]))
+        add_turned(sums[0], fetch_weighed(0, 0, 0))
+        add_turned(sums[1], fetch_weighed(1, 0, 0))
+        add_turned(sums[0], weigh(fetch(0, 0, 1), 0, 0, 1, 1.0), last=True)
+        near10 = fetch(1, 0, 1)
+        add_late(fetch_weighed(0, 1, 0))
+        add_turned(sums[1], weigh(near10, 1, 0, 1, 1.0), last=True)
+        add_late(weigh(fetch(0, 1, 1), 0, 1, 1, 1.0), last=True)
         near11 = fetch(1, 1, 0)
         slope11 = make_slope(1, 1)
+        second11 = narrow("second11")
+        def fetch_last(c):
+            start = HALF + c * P
+            nc.vector.tensor_tensor(second11[:, c * P : (c + 1) * P], y[1][:].indirect(pos_sb[1][:, start // 16 : (start + P) // 16]), gate_sb[:, 1, start : start + P], ALU.mult)
+        fetch_last(0)
         first11 = weigh(near11, 1, 1, 0, 0.5)
-        back00 = turn_back(sums[0, 0], 0, 0, "bank00", "near011")
-        back10 = turn_back(sums[1, 0], 1, 0, "bank10", "near110")
-        back01 = turn_back(sums[0, 1], 0, 1, "bank01")
+        back00 = turn_back(sums[0], 0, 0, "bank00", "near011")
+        back10 = turn_back(sums[1], 1, 0, "bank10", "near110")
+        late_back = []
+        for c in range(HALF // P):
+            turned = keep.tile([P, P], F32, name=f"late_turned{c}")
+            nc.scalar.activation(turned[:], late[c][:], ACT.Copy, scale=0.5)
+            late_back.append(psum.tile([P, HALF], F32, name=f"late_back{c}", tag=f"bank{c}1"))
+            nc.tensor.transpose(late_back[c][:, :P], turned[:], identity[:])
         curve[0, 1] = square(0, 1, "weighed011")
         own11 = make_own(slope11, 1, 1, "near001")
-        second11 = fetch_weighed(1, 1, 1)
+        fetch_last(1)
         both11 = add_terms(first11, own11, 1, 1)
         finish_turned(back00, curve[0, 0], 0, 0)
         finish_halved(second11, both11, 1, 1)
         finish_turned(back10, curve[1, 0], 1, 0)
-        finish_turned(back01, curve[0, 1], 0, 1)
+        for c in range(HALF // P):
+            result = keep.tile([P, P], F32, name=f"late_result{c}")
+            nc.vector.scalar_tensor_tensor(result[:], curve[0, 1][:, c * P : (c + 1) * P], minus_rate[:, 0:1], late_back[c][:, :P], ALU.mult, ALU.add)
+            nc.sync.dma_start(out[0:P, HALF + c * P : HALF + (c + 1) * P], result[:])

@@ -37,6 +37,7 @@ def tile_picked_ygread_fisher_p_kernel(
 
     with ExitStack() as ctx:
         keep = ctx.enter_context(tc.tile_pool(name="keep", bufs=1))
+        shared = ctx.enter_context(tc.tile_pool(name="shared", bufs=1))
         psum = ctx.enter_context(tc.psum_pool(name="psum", bufs=1))
 
         offs_sb = keep.tile([P, LIST_COLS], U16, name="offs_sb")
@@ -65,6 +66,9 @@ def tile_picked_ygread_fisher_p_kernel(
         nc.sync.dma_start(pos1_sb[:], pos1)
         nc.sync.dma_start(pos2_sb[:], pos2)
         nc.sync.dma_start(gate_sb[:], gate.rearrange("d p s -> p d s"))
+        gate_col = keep.tile([P, HALF // P], F32, name="gate_col")
+        with nc.allow_non_contiguous_dma(reason="one gate for each partition and piece"):
+            nc.sync.dma_start(gate_col[:], gate[1, 0, cols(1)].rearrange("(c p) -> p c", p=P))
 
         minus_rate = keep.tile([P, BLOCKS], F32, name="minus_rate")
         half_rate = keep.tile([P, BLOCKS], F32, name="half_rate")
@@ -73,6 +77,8 @@ def tile_picked_ygread_fisher_p_kernel(
         nc.gpsimd.tensor_scalar(minus_rate[:], rate_sb[:], -1.0, 0.0, ALU.mult, ALU.add)
         nc.gpsimd.tensor_scalar(half_rate[:], rate_sb[:], 0.5, 0.0, ALU.mult, ALU.add)
         nc.gpsimd.tensor_scalar(shift[:], rate_sb[:], 1.0, 0.5, ALU.mult, ALU.add)
+        half_gate = keep.tile([P, HALF // P], F32, name="half_gate")
+        nc.gpsimd.tensor_scalar(half_gate[:], gate_col[:], 0.5, 0.0, ALU.mult, ALU.add)
         nc.gpsimd.memset(centre[:], -0.5)
 
         w_codes = [keep.tile([P, P], U32, name=f"w_codes{b}", align_bytes=64) for b in range(BLOCKS)]
@@ -120,7 +126,11 @@ def tile_picked_ygread_fisher_p_kernel(
 
         pos_sb = [pos1_sb, pos2_sb]
 
+        place = {"near101": 2 * HALF, "turned00": 0, "scaled": 4 * HALF}
+
         def narrow(name, tag=None):
+            if name in place:
+                return shared.tile([P, HALF], F32, name=name, offset=place[name])
             return keep.tile([P, HALF], F32, name=name, tag=tag or name)
 
         def fetch_weighed(b, h, d):
@@ -161,14 +171,15 @@ def tile_picked_ygread_fisher_p_kernel(
 
         def turn_back(bank, b, h, tag, buffer=None):
             turned = narrow(f"turned{b}{h}", buffer)
-            nc.scalar.activation(turned[:], bank[:], ACT.Copy, scale=0.5)
+            nc.scalar.activation(turned[:], bank, ACT.Copy, scale=0.5)
             back = psum.tile([P, HALF], F32, name=f"back{b}{h}", tag=tag)
             for c in range(HALF // P):
                 nc.tensor.transpose(back[:, c * P : (c + 1) * P], turned[:, c * P : (c + 1) * P], identity[:])
             return back
 
         def store(result, b, h):
-            nc.sync.dma_start(out[b * P : (b + 1) * P, cols(h)], result[:])
+            queue = nc.scalar if (b, h) in ((1, 1), (0, 1)) else nc.sync
+            queue.dma_start(out[b * P : (b + 1) * P, cols(h)], result[:])
 
         def finish_turned(back, curve, b, h):
             result = narrow(f"result{b}{h}")
@@ -197,23 +208,21 @@ def tile_picked_ygread_fisher_p_kernel(
             nc.vector.scalar_tensor_tensor(result[:], term[:], 0.5, rest[:], ALU.mult, ALU.add)
             store(result, b, h)
 
-        sums = {b: psum.tile([P, HALF], F32, name=f"sum{b}") for b in range(BLOCKS)}
-        late = [psum.tile([P, P], F32, name=f"late{c}") for c in range(HALF // P)]
-        def add_late(term, first=False, last=False):
-            for c in range(HALF // P):
-                nc.tensor.matmul(late[c][:], term[:, c * P : (c + 1) * P], identity[:], start=first, stop=last, is_transpose=True)
+        sums = {q: psum.tile([P, HALF], F32, name=f"sum{q[0]}{q[1]}")[:] for q in ((1, 0), (0, 1))}
+        first_bank = psum.tile([P, S], F32, name="first_bank")
+        sums[0, 0], raw = first_bank[:, cols(0)], first_bank[:, cols(1)]
         curve = {(b, 0): bend(b, 0) for b in range(BLOCKS)}
         for b in range(BLOCKS):
-            add_turned(sums[b], y[b][:, cols(0)], first=True)
-        add_late(y[0][:, cols(1)], first=True)
-        add_late(half_rate[:, 0:1].to_broadcast([P, HALF]))
-        add_turned(sums[0], fetch_weighed(0, 0, 0))
-        add_turned(sums[1], fetch_weighed(1, 0, 0))
-        add_turned(sums[0], weigh(fetch(0, 0, 1), 0, 0, 1, 1.0), last=True)
+            add_turned(sums[b, 0], y[b][:, cols(0)], first=True)
+        add_turned(sums[0, 1], y[0][:, cols(1)], first=True)
+        add_turned(sums[0, 1], half_rate[:, 0:1].to_broadcast([P, HALF]))
+        add_turned(sums[0, 0], fetch_weighed(0, 0, 0))
+        add_turned(sums[1, 0], fetch_weighed(1, 0, 0))
+        add_turned(sums[0, 0], weigh(fetch(0, 0, 1), 0, 0, 1, 1.0))
         near10 = fetch(1, 0, 1)
-        add_late(fetch_weighed(0, 1, 0))
-        add_turned(sums[1], weigh(near10, 1, 0, 1, 1.0), last=True)
-        add_late(weigh(fetch(0, 1, 1), 0, 1, 1, 1.0), last=True)
+        add_turned(raw, fetch(0, 1, 1), last=True)
+        add_turned(sums[0, 1], fetch_weighed(0, 1, 0), last=True)
+        add_turned(sums[1, 0], weigh(near10, 1, 0, 1, 1.0), last=True)
         near11 = fetch(1, 1, 0)
         slope11 = make_slope(1, 1)
         second11 = narrow("second11")
@@ -222,22 +231,21 @@ def tile_picked_ygread_fisher_p_kernel(
             nc.vector.tensor_tensor(second11[:, c * P : (c + 1) * P], y[1][:].indirect(pos_sb[1][:, start // 16 : (start + P) // 16]), gate_sb[:, 1, start : start + P], ALU.mult)
         fetch_last(0)
         first11 = weigh(near11, 1, 1, 0, 0.5)
-        back00 = turn_back(sums[0], 0, 0, "bank00", "near011")
-        back10 = turn_back(sums[1], 1, 0, "bank10", "near110")
-        late_back = []
+        back00 = turn_back(sums[0, 0], 0, 0, "bank00")
+        scaled = narrow("scaled")
         for c in range(HALF // P):
-            turned = keep.tile([P, P], F32, name=f"late_turned{c}")
-            nc.scalar.activation(turned[:], late[c][:], ACT.Copy, scale=0.5)
-            late_back.append(psum.tile([P, HALF], F32, name=f"late_back{c}", tag=f"bank{c}1"))
-            nc.tensor.transpose(late_back[c][:, :P], turned[:], identity[:])
-        curve[0, 1] = square(0, 1, "weighed011")
+            nc.scalar.activation(scaled[:, c * P : (c + 1) * P], raw[:, c * P : (c + 1) * P], ACT.Copy, scale=half_gate[:, c : c + 1])
+        back01 = psum.tile([P, HALF], F32, name="back01", tag="bank01")
+        add_turned(back01, scaled, first=True)
+        back10 = turn_back(sums[1, 0], 1, 0, "bank10")
+        turned01 = narrow("turned01", "near110")
+        nc.scalar.activation(turned01[:], sums[0, 1], ACT.Copy, scale=0.5)
+        add_turned(back01, turned01, last=True)
+        curve[0, 1] = square(0, 1, "weighed101")
         own11 = make_own(slope11, 1, 1, "near001")
         fetch_last(1)
         both11 = add_terms(first11, own11, 1, 1)
         finish_turned(back00, curve[0, 0], 0, 0)
         finish_halved(second11, both11, 1, 1)
         finish_turned(back10, curve[1, 0], 1, 0)
-        for c in range(HALF // P):
-            result = keep.tile([P, P], F32, name=f"late_result{c}")
-            nc.vector.scalar_tensor_tensor(result[:], curve[0, 1][:, c * P : (c + 1) * P], minus_rate[:, 0:1], late_back[c][:, :P], ALU.mult, ALU.add)
-            nc.sync.dma_start(out[0:P, HALF + c * P : HALF + (c + 1) * P], result[:])
+        finish_turned(back01, curve[0, 1], 0, 1)

@@ -77,8 +77,6 @@ def tile_picked_ygread_fisher_p_kernel(
         nc.gpsimd.tensor_scalar(minus_rate[:], rate_sb[:], -1.0, 0.0, ALU.mult, ALU.add)
         nc.gpsimd.tensor_scalar(half_rate[:], rate_sb[:], 0.5, 0.0, ALU.mult, ALU.add)
         nc.gpsimd.tensor_scalar(shift[:], rate_sb[:], 1.0, 0.5, ALU.mult, ALU.add)
-        half_gate = keep.tile([P, HALF // P], F32, name="half_gate")
-        nc.gpsimd.tensor_scalar(half_gate[:], gate_col[:], 0.5, 0.0, ALU.mult, ALU.add)
         nc.gpsimd.memset(centre[:], -0.5)
 
         w_codes = [keep.tile([P, P], U32, name=f"w_codes{b}", align_bytes=64) for b in range(BLOCKS)]
@@ -138,9 +136,9 @@ def tile_picked_ygread_fisher_p_kernel(
             nc.vector.tensor_tensor(dst[:], y[b][:].indirect(pos_sb[d][:, entries(h)]), gate_sb[:, d, cols(h)], ALU.mult)
             return dst
 
-        def fetch(b, h, d, tag=None):
+        def fetch(b, h, d, tag=None, scale=1.0):
             dst = narrow(f"near{b}{h}{d}", tag)
-            nc.scalar.activation(dst[:], y[b][:].indirect(pos_sb[d][:, entries(h)]), ACT.Copy)
+            nc.scalar.activation(dst[:], y[b][:].indirect(pos_sb[d][:, entries(h)]), ACT.Copy, scale=scale)
             return dst
 
         def weigh(near, b, h, d, factor):
@@ -178,8 +176,7 @@ def tile_picked_ygread_fisher_p_kernel(
             return back
 
         def store(result, b, h):
-            queue = nc.scalar if (b, h) in ((1, 1), (0, 1)) else nc.sync
-            queue.dma_start(out[b * P : (b + 1) * P, cols(h)], result[:])
+            nc.sync.dma_start(out[b * P : (b + 1) * P, cols(h)], result[:])
 
         def finish_turned(back, curve, b, h):
             result = narrow(f"result{b}{h}")
@@ -220,7 +217,7 @@ def tile_picked_ygread_fisher_p_kernel(
         add_turned(sums[1, 0], fetch_weighed(1, 0, 0))
         add_turned(sums[0, 0], weigh(fetch(0, 0, 1), 0, 0, 1, 1.0))
         near10 = fetch(1, 0, 1)
-        add_turned(raw, fetch(0, 1, 1), last=True)
+        add_turned(raw, fetch(0, 1, 1, scale=0.5), last=True)
         add_turned(sums[0, 1], fetch_weighed(0, 1, 0), last=True)
         add_turned(sums[1, 0], weigh(near10, 1, 0, 1, 1.0), last=True)
         near11 = fetch(1, 1, 0)
@@ -234,7 +231,7 @@ def tile_picked_ygread_fisher_p_kernel(
         back00 = turn_back(sums[0, 0], 0, 0, "bank00")
         scaled = narrow("scaled")
         for c in range(HALF // P):
-            nc.scalar.activation(scaled[:, c * P : (c + 1) * P], raw[:, c * P : (c + 1) * P], ACT.Copy, scale=half_gate[:, c : c + 1])
+            nc.scalar.activation(scaled[:, c * P : (c + 1) * P], raw[:, c * P : (c + 1) * P], ACT.Copy, scale=gate_col[:, c : c + 1])
         back01 = psum.tile([P, HALF], F32, name="back01", tag="bank01")
         add_turned(back01, scaled, first=True)
         back10 = turn_back(sums[1, 0], 1, 0, "bank10")

@@ -43,7 +43,7 @@ def tile_picked_ygread_fisher_p_kernel(
         offs_sb = keep.tile([P, LIST_COLS], U16, name="offs_sb")
         pos1_sb = keep.tile([P, LIST_COLS], U16, name="pos1_sb")
         pos2_sb = keep.tile([P, LIST_COLS], U16, name="pos2_sb")
-        table_scales = keep.tile([P, T], U8, name="table_scales", align_bytes=64)
+        table_scales = shared.tile([P, T], U8, name="table_scales", align_bytes=64, offset=8 * HALF)
         table_words = keep.tile([P, T], I32, name="table_words", align_bytes=64)
         w_raw = keep.tile([P, PACK, N], F32, name="w_raw")
         identity = keep.tile([P, P], F32, name="identity")
@@ -79,7 +79,10 @@ def tile_picked_ygread_fisher_p_kernel(
         nc.gpsimd.tensor_scalar(shift[:], rate_sb[:], 1.0, 0.5, ALU.mult, ALU.add)
         nc.gpsimd.memset(centre[:], -0.5)
 
-        w_codes = [keep.tile([P, P], U32, name=f"w_codes{b}", align_bytes=64) for b in range(BLOCKS)]
+        w_codes = [
+            keep.tile([P, P], U32, name="w_codes0", align_bytes=64),
+            shared.tile([P, P], U32, name="w_codes1", align_bytes=64, offset=8 * HALF),
+        ]
         w_scales = [keep.tile([P, P], U8, name=f"w_scales{b}", align_bytes=64) for b in range(BLOCKS)]
         w_grouped = [keep.tile([P, P, PACK], BF16, name=f"w_grouped{b}", align_bytes=64) for b in range(BLOCKS)]
 
@@ -98,10 +101,10 @@ def tile_picked_ygread_fisher_p_kernel(
 
         round_weights(0, nc.vector.tensor_copy)
         round_weights(1, nc.scalar.copy)
+        quantize_weights(0)
         picked_scales = keep.tile([P, S], U8, name="picked_scales", align_bytes=64)
         nc.vector.tensor_copy(picked_scales[:], table_scales[:].indirect(offs_sb[:]))
-        for b in range(BLOCKS):
-            quantize_weights(b)
+        quantize_weights(1)
 
         picked_words = [keep.tile([P, HALF], U32, name=f"picked_words{h}", align_bytes=64) for h in range(HALVES)]
         for h in range(HALVES):

from contextlib import ExitStack

import concourse.mybir as mybir
from concourse.masks import make_identity

K, T, S, N = 512, 2048, 512, 256
FLOPS = 2 * K * N * S

F32 = mybir.dt.float32
BF16 = mybir.dt.bfloat16
I32 = mybir.dt.int32
U32 = mybir.dt.uint32
U16 = mybir.dt.uint16
U8 = mybir.dt.uint8
FP8X4 = mybir.dt.float8_e4m3fn_x4
ALU = mybir.AluOpType
ACT = mybir.ActivationFunctionType

P = 128
PACK = 4
LIST_COLS = S // 16
BLOCKS = N // P
HALVES = 2
HALF = S // HALVES


def tile_picked_ygread_fisher_p_kernel(
    tc, x_words, x_scales, w1, gate, rate, offs, pos1, pos2, out
):
    nc = tc.nc

    def cols(h):
        return slice(h * HALF, (h + 1) * HALF)

    def entries(h):
        return slice(h * HALF // 16, (h + 1) * HALF // 16)

    with ExitStack() as ctx:
        keep = ctx.enter_context(tc.tile_pool(name="keep", bufs=1))
        shared = ctx.enter_context(tc.tile_pool(name="shared", bufs=1))
        psum = ctx.enter_context(tc.psum_pool(name="psum", bufs=1))

        offs_sb = keep.tile([P, LIST_COLS], U16, name="offs_sb")
        pos1_sb = keep.tile([P, LIST_COLS], U16, name="pos1_sb")
        pos2_sb = keep.tile([P, LIST_COLS], U16, name="pos2_sb")
        table_scales = shared.tile([P, T], U8, name="table_scales", align_bytes=64, offset=8 * HALF)
        table_words = keep.tile([P, T], I32, name="table_words", align_bytes=64)
        w_raw = keep.tile([P, PACK, N], F32, name="w_raw")
        identity = keep.tile([P, P], F32, name="identity")
        gate_sb = keep.tile([P, 2, S], F32, name="gate_sb")
        rate_sb = keep.tile([P, BLOCKS], F32, name="rate_sb")

        nc.vector.memset(table_scales[:].bitcast(I32), 0)
        nc.vector.memset(identity[:], 0.0)
        make_identity(nc, identity[:], nomemset=True)
        nc.sync.dma_start(w_raw[:], w1.rearrange("(p j) m -> p j m", j=PACK))
        nc.sync.dma_start(offs_sb[:], offs)
        for q in range(4):
            nc.sync.dma_start(
                table_scales[32 * q : 32 * q + 4, :].bitcast(I32),
                x_scales[0, 4 * q : 4 * q + 4, :].bitcast(I32),
            )
        nc.sync.dma_start(table_words[:], x_words[0].rearrange("p c r -> p (c r)").bitcast(I32))
        with nc.allow_non_contiguous_dma(reason="one rate for each partition and block"):
            nc.sync.dma_start(rate_sb[:], rate.rearrange("(b p) o -> p (b o)", p=P))
        nc.sync.dma_start(pos1_sb[:], pos1)
        nc.sync.dma_start(pos2_sb[:], pos2)
        nc.sync.dma_start(gate_sb[:], gate.rearrange("d p s -> p d s"))
        gate_col = keep.tile([P, HALF // P], F32, name="gate_col")
        with nc.allow_non_contiguous_dma(reason="one gate for each partition and piece"):
            nc.sync.dma_start(gate_col[:], gate[1, 0, cols(1)].rearrange("(c p) -> p c", p=P))

        minus_rate = keep.tile([P, BLOCKS], F32, name="minus_rate")
        half_rate = keep.tile([P, BLOCKS], F32, name="half_rate")
        shift = keep.tile([P, BLOCKS], F32, name="shift")
        centre = keep.tile([P, 1], F32, name="centre")
        nc.gpsimd.tensor_scalar(minus_rate[:], rate_sb[:], -1.0, 0.0, ALU.mult, ALU.add)
        nc.gpsimd.tensor_scalar(half_rate[:], rate_sb[:], 0.5, 0.0, ALU.mult, ALU.add)
        nc.gpsimd.tensor_scalar(shift[:], rate_sb[:], 1.0, 0.5, ALU.mult, ALU.add)
        nc.gpsimd.memset(centre[:], -0.5)

        w_codes = [
            keep.tile([P, P], U32, name="w_codes0", align_bytes=64),
            shared.tile([P, P], U32, name="w_codes1", align_bytes=64, offset=8 * HALF),
        ]
        w_scales = [keep.tile([P, P], U8, name=f"w_scales{b}", align_bytes=64) for b in range(BLOCKS)]
        w_grouped = [keep.tile([P, P, PACK], BF16, name=f"w_grouped{b}", align_bytes=64) for b in range(BLOCKS)]

        def round_weights(b, copy):
            copy(
                w_grouped[b][:].rearrange("p (c i) j -> p c j i", i=4),
                w_raw[:, :, b * P : (b + 1) * P].rearrange("p j (c i) -> p c j i", i=4),
            )

        def quantize_weights(b):
            nc.vector.quantize_mx(
                out=w_codes[b][:].bitcast(FP8X4),
                scales=w_scales[b][:],
                in_=w_grouped[b][:].rearrange("p m j -> p (m j)"),
            )

        round_weights(0, nc.vector.tensor_copy)
        round_weights(1, nc.scalar.copy)
        quantize_weights(0)
        picked_scales = keep.tile([P, S], U8, name="picked_scales", align_bytes=64)
        nc.vector.tensor_copy(picked_scales[:], table_scales[:].indirect(offs_sb[:]))
        quantize_weights(1)

        picked_words = [keep.tile([P, HALF], U32, name=f"picked_words{h}", align_bytes=64) for h in range(HALVES)]
        for h in range(HALVES):
            nc.vector.tensor_copy(picked_words[h][:], table_words[:].bitcast(U32).indirect(offs_sb[:, entries(h)]))

        y = [keep.tile([P, S], F32, name=f"y{b}") for b in range(BLOCKS)]
        for h in range(HALVES):
            for b in range(BLOCKS):
                acc = psum.tile([P, HALF], F32, name=f"acc{b}{h}", tag=f"bank{b}{h}")
                nc.tensor.matmul_mx(
                    out=acc[:],
                    lhsT=w_codes[b][:].bitcast(FP8X4),
                    lhsT_scale=w_scales[b][:],
                    rhs=picked_words[h][:].bitcast(FP8X4),
                    rhs_scale=picked_scales[:, cols(h)],
                    start=True,
                    stop=True,
                )
                nc.scalar.activation(y[b][:, cols(h)], acc[:], ACT.Sigmoid)

        pos_sb = [pos1_sb, pos2_sb]

        place = {"near101": 2 * HALF, "turned00": 0, "scaled": 4 * HALF}

        def narrow(name, tag=None):
            if name in place:
                return shared.tile([P, HALF], F32, name=name, offset=place[name])
            return keep.tile([P, HALF], F32, name=name, tag=tag or name)

        def fetch_weighed(b, h, d):
            dst = narrow(f"weighed{b}{h}{d}")
            nc.vector.tensor_tensor(dst[:], y[b][:].indirect(pos_sb[d][:, entries(h)]), gate_sb[:, d, cols(h)], ALU.mult)
            return dst

        def fetch(b, h, d, tag=None, scale=1.0):
            dst = narrow(f"near{b}{h}{d}", tag)
            nc.scalar.activation(dst[:], y[b][:].indirect(pos_sb[d][:, entries(h)]), ACT.Copy, scale=scale)
            return dst

        def weigh(near, b, h, d, factor):
            dst = narrow(f"weighed{b}{h}{d}")
            nc.vector.scalar_tensor_tensor(dst[:], near[:], factor, gate_sb[:, d, cols(h)], ALU.mult, ALU.mult)
            return dst

        def bend(b, h):
            dst = narrow(f"bend{b}{h}")
            nc.vector.scalar_tensor_tensor(dst[:], y[b][:, cols(h)], -1.0, y[b][:, cols(h)], ALU.add, ALU.mult)
            return dst

        def square(b, h, tag=None):
            dst = narrow(f"square{b}{h}", tag)
            nc.scalar.activation(dst[:], y[b][:, cols(h)], ACT.Square, bias=centre[:])
            return dst

        def add_turned(bank, term, first=False, last=False):
            for c in range(HALF // P):
                nc.tensor.matmul(
                    bank[:, c * P : (c + 1) * P],
                    term[:, c * P : (c + 1) * P],
                    identity[:],
                    start=(first and c == 0),
                    stop=(last and c == HALF // P - 1),
                    is_transpose=True,
                )

        def turn_back(bank, b, h, tag, buffer=None):
            turned = narrow(f"turned{b}{h}", buffer)
            nc.scalar.activation(turned[:], bank, ACT.Copy, scale=0.5)
            back = psum.tile([P, HALF], F32, name=f"back{b}{h}", tag=tag)
            for c in range(HALF // P):
                nc.tensor.transpose(back[:, c * P : (c + 1) * P], turned[:, c * P : (c + 1) * P], identity[:])
            return back

        def store(result, b, h):
            nc.sync.dma_start(out[b * P : (b + 1) * P, cols(h)], result[:])

        def finish_turned(back, curve, b, h):
            result = narrow(f"result{b}{h}")
            nc.vector.scalar_tensor_tensor(result[:], curve[:], minus_rate[:, b : b + 1], back[:], ALU.mult, ALU.add)
            store(result, b, h)

        def make_slope(b, h, tag=None):
            dst = narrow(f"slope{b}{h}", tag)
            nc.scalar.activation(
                dst[:], y[b][:, cols(h)], ACT.Identity, bias=shift[:, b : b + 1], scale=minus_rate[:, b : b + 1]
            )
            return dst

        def make_own(slope, b, h, tag=None):
            dst = narrow(f"own{b}{h}", tag)
            nc.vector.tensor_tensor(dst[:], slope[:], y[b][:, cols(h)], ALU.mult)
            return dst

        def add_terms(first, second, b, h, tag=None):
            dst = narrow(f"both{b}{h}", tag)
            nc.vector.tensor_tensor(dst[:], first[:], second[:], ALU.add)
            return dst

        def finish_halved(term, rest, b, h):
            result = narrow(f"result{b}{h}")
            nc.vector.scalar_tensor_tensor(result[:], term[:], 0.5, rest[:], ALU.mult, ALU.add)
            store(result, b, h)

        sums = {q: psum.tile([P, HALF], F32, name=f"sum{q[0]}{q[1]}")[:] for q in ((1, 0), (0, 1))}
        first_bank = psum.tile([P, S], F32, name="first_bank")
        sums[0, 0], raw = first_bank[:, cols(0)], first_bank[:, cols(1)]
        curve = {(b, 0): bend(b, 0) for b in range(BLOCKS)}
        for b in range(BLOCKS):
            add_turned(sums[b, 0], y[b][:, cols(0)], first=True)
        add_turned(sums[0, 1], y[0][:, cols(1)], first=True)
        add_turned(sums[0, 1], half_rate[:, 0:1].to_broadcast([P, HALF]))
        add_turned(sums[0, 0], fetch_weighed(0, 0, 0))
        add_turned(sums[1, 0], fetch_weighed(1, 0, 0))
        add_turned(sums[0, 0], weigh(fetch(0, 0, 1), 0, 0, 1, 1.0))
        near10 = fetch(1, 0, 1)
        add_turned(raw, fetch(0, 1, 1, scale=0.5), last=True)
        add_turned(sums[0, 1], fetch_weighed(0, 1, 0), last=True)
        add_turned(sums[1, 0], weigh(near10, 1, 0, 1, 1.0), last=True)
        near11 = fetch(1, 1, 0)
        slope11 = make_slope(1, 1)
        second11 = narrow("second11")
        def fetch_last(c):
            start = HALF + c * P
            nc.vector.tensor_tensor(second11[:, c * P : (c + 1) * P], y[1][:].indirect(pos_sb[1][:, start // 16 : (start + P) // 16]), gate_sb[:, 1, start : start + P], ALU.mult)
        fetch_last(0)
        first11 = weigh(near11, 1, 1, 0, 0.5)
        back00 = turn_back(sums[0, 0], 0, 0, "bank00")
        scaled = narrow("scaled")
        for c in range(HALF // P):
            nc.scalar.activation(scaled[:, c * P : (c + 1) * P], raw[:, c * P : (c + 1) * P], ACT.Copy, scale=gate_col[:, c : c + 1])
        back01 = psum.tile([P, HALF], F32, name="back01", tag="bank01")
        add_turned(back01, scaled, first=True)
        back10 = turn_back(sums[1, 0], 1, 0, "bank10")
        turned01 = narrow("turned01", "near110")
        nc.scalar.activation(turned01[:], sums[0, 1], ACT.Copy, scale=0.5)
        add_turned(back01, turned01, last=True)
        curve[0, 1] = square(0, 1, "weighed101")
        own11 = make_own(slope11, 1, 1, "near001")
        fetch_last(1)
        both11 = add_terms(first11, own11, 1, 1)
        finish_turned(back00, curve[0, 0], 0, 0)
        finish_halved(second11, both11, 1, 1)
        finish_turned(back10, curve[1, 0], 1, 0)
        finish_turned(back01, curve[0, 1], 0, 1)
